import numpy as np, ml_dtypes
CORES = [6,14,30,38,62,70,86,94,102]
N = 9
GR, GC, TK = 3, 3, 512
RA = [[2,-1,-2],[2,2,2],[-1,1,-1]]
CB = [[-1,-2,2],[-1,-1,-2],[1,2,1]]
def setup_inputs(rng):
    return {"x": rng.standard_normal((N, 128, TK), dtype=np.float32).astype(ml_dtypes.bfloat16), "a": (rng.standard_normal((N, 128, 128), dtype=np.float32) / 11).astype(ml_dtypes.bfloat16)}
def setup_inputs_big(rng):
    d = setup_inputs(rng)
    for k in ("x", "a"): d[k] = (d[k].astype(np.float32) * 1024.0).astype(d[k].dtype)
    return d
def setup_inputs_small(rng):
    d = setup_inputs(rng)
    for k in ("x", "a"): d[k] = (d[k].astype(np.float32) * (1 / 1024.0)).astype(d[k].dtype)
    return d
def setup_inputs_apart(rng):
    d = setup_inputs(rng)
    f = (10.0 ** rng.permutation(np.linspace(-1.5, 1.5, N))).astype(np.float32).reshape(N, 1, 1)
    for k in ("x", "a"): d[k] = (d[k].astype(np.float32) * f).astype(d[k].dtype)
    return d
def reference(x, a):
    X, A = x.astype(np.float64), a.astype(np.float64)
    y = np.zeros((N, 128, TK))
    for i in range(GR):
        for j in range(GC):
            t = sum(RA[i][k] * CB[j][l] * X[k * GC + l] for k in range(GR) for l in range(GC))
            y[i * GC + j] = A[i * GC + j].T @ t
    return {"y": y.astype(ml_dtypes.bfloat16)}

@@ -1,0 +1,177 @@
+import math
+from concourse.bass import DstId, RemoteDMATransfer
+from concourse.mybir import AluOpType
+
+P = 128
+TK = 512
+G = 3
+NCH = 1
+W = TK // NCH
+NA = 2 * G - 1
+
+SCRATCH = {
+    "xs": ("sbuf", [P, G * TK], "bfloat16"),
+    "xo": ("sbuf", [P, TK], "bfloat16"),
+    "cx": ("sbuf", [P, TK], "bfloat16"),
+    "vs": ("sbuf", [P, G * TK], "bfloat16"),
+    "a0": ("sbuf", [P, P], "bfloat16"),
+    "ca": ("sbuf", [P, NA * P], "bfloat16"),
+    "sa": ("sbuf", [P, NA * P], "bfloat16"),
+    "yb": ("sbuf", [P, TK], "bfloat16"),
+}
+for _c in range(NCH):
+    SCRATCH["ps%d" % _c] = ("psum", [P, 512], "float32")
+
+SEMAPHORES = ["lda", "fill", "asc", "sent"]
+for _c in range(NCH):
+    SEMAPHORES += ["ldx%d" % _c, "xo%d" % _c, "p1c%d" % _c, "mm%d" % _c, "cp%d" % _c, "st%d" % _c]
+    SEMAPHORES += ["v%dc%d" % (_l, _c) for _l in range(G)]
+
+
+def _perms(n):
+    if n == 0:
+        return [[]]
+    return [p[:q] + [n - 1] + p[q:] for p in _perms(n - 1) for q in range(n)]
+
+
+def _plan(RA):
+    n = len(RA)
+    best = None
+    for p in _perms(n):
+        ok = True
+        for k in range(n):
+            oth = [RA[p[k]][m] for m in range(n) if m != k and RA[p[k]][m] != 0]
+            if not oth or min(oth) < 0 < max(oth):
+                ok = False
+        home = sum(1 for k in range(n) if p[k] == k)
+        if ok and (best is None or home > best[0]):
+            best = (home, p)
+    assert best is not None
+    folds = best[1]
+    scale = [0] * n
+    for k in range(n):
+        oth = [RA[folds[k]][m] for m in range(n) if m != k and RA[folds[k]][m] != 0]
+        d = 0
+        for v in oth:
+            d = math.gcd(d, abs(v))
+        scale[folds[k]] = d if oth[0] > 0 else -d
+    return folds, scale
+
+
+def rank_program(g, core, T, topo):
+    rank = T.rank_of(core)
+    if rank is None:
+        return
+    RA, CB = T.tables["RA"], T.tables["CB"]
+    S = T.sem
+    k, l = rank // G, rank % G
+    folds, scale = _plan(RA)
+    tgt = folds[k]
+    s_t = scale[tgt]
+    own_f = RA[tgt][k] / s_t
+    s_k = scale[k]
+
+    def blk(slot, c):
+        return slice(slot * TK + c * W, slot * TK + (c + 1) * W)
+
+    def two_dests(ranks, srcs, dst_ap, sem, alu):
+        cores = [T.cores[r] for r in ranks]
+        mask = -1
+        for d in cores:
+            assert topo.may_write(core, d)
+            mask &= topo.mask(core, d)
+        ids = [DstId(rid=topo.addr(d)[0], pnc=topo.addr(d)[1]) for d in cores]
+        tr = RemoteDMATransfer(dst_ids=ids, dma_engine_mask=mask, remote_sem=sem, srcs=srcs,
+                               dsts=[dst_ap for _ in cores], alu_op=alu)
+        g.remote_dma_fused([tr], local_sem=S.sent)
+        return bin(mask).count("1")
+
+    def eng(src_rank):
+        return bin(topo.mask(T.cores[src_rank], core)).count("1")
+
+    col_others = [m for m in range(G) if m != k]
+    row_others = [j for j in range(G) if j != l]
+    src_row = folds.index(k)
+    p1_total = sum(eng(m * G + l) for m in col_others)
+
+    own_terms = [(RA[k][m] * CB[l][l], m) for m in range(G) if RA[k][m] * CB[l][l] != 0]
+    in_terms = [(CB[l][j] * s_k, j) for j in row_others]
+    factors = []
+    for f, _ in own_terms + in_terms:
+        if f != 1 and f not in factors:
+            factors.append(f)
+
+    def a_times(f):
+        if f == 1:
+            return T.a0[:]
+        q = factors.index(f)
+        return T.sa[:, q * P:(q + 1) * P]
+
+    ldq = [g.sync, g.scalar]
+    for c in range(NCH):
+        ldq[c % 2].dma_start(T.xs[:, blk(k, c)], T.x[:, c * W:(c + 1) * W]).then_inc(S["ldx%d" % c], 16)
+    ldq[NCH % 2].dma_start(T.a0[:], T.a[:]).then_inc(S.lda, 16)
+
+    V = g.vector
+    fills = 0
+    if own_f not in (0, 1):
+        V.memset(T.cx[:], own_f).then_inc(S.fill, 1)
+        fills += 1
+    for q, f in enumerate(factors):
+        V.memset(T.ca[:, q * P:(q + 1) * P], f).then_inc(S.fill, 1)
+        fills += 1
+    if fills:
+        V.wait_ge(S.fill, fills)
+    if own_f not in (0, 1):
+        for c in range(NCH):
+            V.wait_ge(S["ldx%d" % c], 16)
+            V.tensor_tensor(T.xo[:, c * W:(c + 1) * W], T.xs[:, blk(k, c)], T.cx[:, c * W:(c + 1) * W],
+                            AluOpType.mult).then_inc(S["xo%d" % c], 1)
+    V.wait_ge(S.lda, 16)
+    for q, f in enumerate(factors):
+        V.tensor_tensor(T.sa[:, q * P:(q + 1) * P], T.a0[:], T.ca[:, q * P:(q + 1) * P],
+                        AluOpType.mult).then_inc(S.asc, 1)
+
+    sent = 0
+    for c in range(NCH):
+        g.wait_ge(S["ldx%d" % c], 16)
+        sent += two_dests([m * G + l for m in col_others], [T.xs[:, blk(k, c)]], T.xs[:, blk(k, c)],
+                          S["p1c%d" % c], 0)
+    for c in range(NCH):
+        g.wait_ge(S["p1c%d" % c], p1_total)
+        srcs = []
+        if own_f == 1:
+            srcs.append(T.xs[:, blk(k, c)])
+        elif own_f != 0:
+            g.wait_ge(S["xo%d" % c], 1)
+            srcs.append(T.xo[:, c * W:(c + 1) * W])
+        for m in col_others:
+            srcs += [T.xs[:, blk(m, c)]] * (RA[tgt][m] // s_t)
+        sent += two_dests([tgt * G + j for j in row_others], srcs, T.vs[:, blk(l, c)], S["v%dc%d" % (l, c)], 1)
+
+    TE = g.tensor
+    TE.wait_ge(S.lda, 16)
+    if factors:
+        TE.wait_ge(S.asc, len(factors))
+    for c in range(NCH):
+        ps = T["ps%d" % c]
+        TE.wait_ge(S["ldx%d" % c], 16)
+        TE.wait_ge(S["p1c%d" % c], p1_total)
+        for n, (f, m) in enumerate(own_terms):
+            TE.matmul(ps[:, 0:W], a_times(f), T.xs[:, blk(m, c)], n == 0, False)
+    for c in range(NCH):
+        ps = T["ps%d" % c]
+        for n, (f, j) in enumerate(in_terms):
+            TE.wait_ge(S["v%dc%d" % (j, c)], eng(src_row * G + j))
+            mm = TE.matmul(ps[:, 0:W], a_times(f), T.vs[:, blk(j, c)], False, n == len(in_terms) - 1)
+        mm.then_inc(S["mm%d" % c], 1)
+
+    for c in range(NCH):
+        V.wait_ge(S["mm%d" % c], 1)
+        V.tensor_copy(T.yb[:, c * W:(c + 1) * W], T["ps%d" % c][:, 0:W]).then_inc(S["cp%d" % c], 1)
+        q = ldq[c % 2]
+        q.wait_ge(S["cp%d" % c], 1)
+        q.dma_start(T.y[:, c * W:(c + 1) * W], T.yb[:, c * W:(c + 1) * W]).then_inc(S["st%d" % c], 16)
+    g.wait_ge(S.sent, sent)
+    for c in range(NCH):
+        g.wait_ge(S["st%d" % c], 16)

@@ -1,61 +1,33 @@
-import math
 from concourse.bass import DstId, RemoteDMATransfer
 from concourse.mybir import AluOpType
 
 P = 128
 TK = 512
 G = 3
-NCH = 1
-W = TK // NCH
-NA = 2 * G - 1
+NQ = 4
+CW = TK // NQ
 
 SCRATCH = {
+    "xd": ("dram", [P, TK], "bfloat16"),
     "xs": ("sbuf", [P, G * TK], "bfloat16"),
-    "xo": ("sbuf", [P, TK], "bfloat16"),
-    "cx": ("sbuf", [P, TK], "bfloat16"),
     "vs": ("sbuf", [P, G * TK], "bfloat16"),
+    "on": ("sbuf", [P, P], "bfloat16"),
+    "idn": ("sbuf", [P, P], "bfloat16"),
+    "ci": ("sbuf", [P, G * P], "bfloat16"),
+    "si": ("sbuf", [P, G * P], "bfloat16"),
     "a0": ("sbuf", [P, P], "bfloat16"),
-    "ca": ("sbuf", [P, NA * P], "bfloat16"),
-    "sa": ("sbuf", [P, NA * P], "bfloat16"),
+    "ca": ("sbuf", [P, G * P], "bfloat16"),
+    "sa": ("sbuf", [P, G * P], "bfloat16"),
     "yb": ("sbuf", [P, TK], "bfloat16"),
 }
-for _c in range(NCH):
+for _c in range(NQ):
+    SCRATCH["pv%d" % _c] = ("psum", [P, 512], "float32")
     SCRATCH["ps%d" % _c] = ("psum", [P, 512], "float32")
 
-SEMAPHORES = ["lda", "fill", "asc", "sent"]
-for _c in range(NCH):
-    SEMAPHORES += ["ldx%d" % _c, "xo%d" % _c, "p1c%d" % _c, "mm%d" % _c, "cp%d" % _c, "st%d" % _c]
-    SEMAPHORES += ["v%dc%d" % (_l, _c) for _l in range(G)]
-
-
-def _perms(n):
-    if n == 0:
-        return [[]]
-    return [p[:q] + [n - 1] + p[q:] for p in _perms(n - 1) for q in range(n)]
-
-
-def _plan(RA):
-    n = len(RA)
-    best = None
-    for p in _perms(n):
-        ok = True
-        for k in range(n):
-            oth = [RA[p[k]][m] for m in range(n) if m != k and RA[p[k]][m] != 0]
-            if not oth or min(oth) < 0 < max(oth):
-                ok = False
-        home = sum(1 for k in range(n) if p[k] == k)
-        if ok and (best is None or home > best[0]):
-            best = (home, p)
-    assert best is not None
-    folds = best[1]
-    scale = [0] * n
-    for k in range(n):
-        oth = [RA[folds[k]][m] for m in range(n) if m != k and RA[folds[k]][m] != 0]
-        d = 0
-        for v in oth:
-            d = math.gcd(d, abs(v))
-        scale[folds[k]] = d if oth[0] > 0 else -d
-    return folds, scale
+SEMAPHORES = ["ldd", "ldx", "lda", "one", "fill", "idy", "isc", "asc", "sent", "p1", "vcp", "cp", "st"]
+SEMAPHORES += ["v%d" % _l for _l in range(G)]
+SEMAPHORES += ["vm%d" % _c for _c in range(NQ)]
+SEMAPHORES += ["mm%d" % _c for _c in range(NQ)]
 
 
 def rank_program(g, core, T, topo):
@@ -65,113 +37,119 @@ def rank_program(g, core, T, topo):
     RA, CB = T.tables["RA"], T.tables["CB"]
     S = T.sem
     k, l = rank // G, rank % G
-    folds, scale = _plan(RA)
-    tgt = folds[k]
-    s_t = scale[tgt]
-    own_f = RA[tgt][k] / s_t
-    s_k = scale[k]
 
-    def blk(slot, c):
-        return slice(slot * TK + c * W, slot * TK + (c + 1) * W)
+    def slot(q):
+        return slice(q * TK, (q + 1) * TK)
 
-    def two_dests(ranks, srcs, dst_ap, sem, alu):
+    def blk(q, c):
+        return slice(q * TK + c * CW, q * TK + (c + 1) * CW)
+
+    def write(ranks, src, dst_ap, sem):
         cores = [T.cores[r] for r in ranks]
         mask = -1
         for d in cores:
             assert topo.may_write(core, d)
             mask &= topo.mask(core, d)
         ids = [DstId(rid=topo.addr(d)[0], pnc=topo.addr(d)[1]) for d in cores]
-        tr = RemoteDMATransfer(dst_ids=ids, dma_engine_mask=mask, remote_sem=sem, srcs=srcs,
-                               dsts=[dst_ap for _ in cores], alu_op=alu)
+        tr = RemoteDMATransfer(dst_ids=ids, dma_engine_mask=mask, remote_sem=sem, srcs=[src],
+                               dsts=[dst_ap for _ in cores], alu_op=0)
         g.remote_dma_fused([tr], local_sem=S.sent)
         return bin(mask).count("1")
 
     def eng(src_rank):
         return bin(topo.mask(T.cores[src_rank], core)).count("1")
 
-    col_others = [m for m in range(G) if m != k]
-    row_others = [j for j in range(G) if j != l]
-    src_row = folds.index(k)
-    p1_total = sum(eng(m * G + l) for m in col_others)
+    col_next = [(k + 1) % G, (k + 2) % G]
+    row_next = [(l + 1) % G, (l + 2) % G]
+    row_from = [(l + G - 1) % G, (l + 1) % G]
+    p1_total = sum(eng(m * G + l) for m in col_next)
 
-    own_terms = [(RA[k][m] * CB[l][l], m) for m in range(G) if RA[k][m] * CB[l][l] != 0]
-    in_terms = [(CB[l][j] * s_k, j) for j in row_others]
-    factors = []
-    for f, _ in own_terms + in_terms:
-        if f != 1 and f not in factors:
-            factors.append(f)
+    ifac, afac = [], []
+    for m in range(G):
+        if RA[k][m] != 1 and RA[k][m] not in ifac:
+            ifac.append(RA[k][m])
+        if CB[l][m] != 1 and CB[l][m] not in afac:
+            afac.append(CB[l][m])
+
+    def i_times(f):
+        if f == 1:
+            return T.idn[:]
+        q = ifac.index(f)
+        return T.si[:, q * P:(q + 1) * P]
 
     def a_times(f):
         if f == 1:
             return T.a0[:]
-        q = factors.index(f)
+        q = afac.index(f)
         return T.sa[:, q * P:(q + 1) * P]
 
-    ldq = [g.sync, g.scalar]
-    for c in range(NCH):
-        ldq[c % 2].dma_start(T.xs[:, blk(k, c)], T.x[:, c * W:(c + 1) * W]).then_inc(S["ldx%d" % c], 16)
-    ldq[NCH % 2].dma_start(T.a0[:], T.a[:]).then_inc(S.lda, 16)
+    g.sync.dma_start(T.xd[:], T.x[:, 0:TK]).then_inc(S.ldd, 16)
+    g.sync.dma_start(T.xs[:, slot(k)], T.x[:, 0:TK]).then_inc(S.ldx, 16)
+    g.sync.dma_start(T.a0[:], T.a[:]).then_inc(S.lda, 16)
 
     V = g.vector
+    V.memset(T.on[:], 1.0).then_inc(S.one, 1)
     fills = 0
-    if own_f not in (0, 1):
-        V.memset(T.cx[:], own_f).then_inc(S.fill, 1)
+    for q, f in enumerate(ifac):
+        V.memset(T.ci[:, q * P:(q + 1) * P], f).then_inc(S.fill, 1)
         fills += 1
-    for q, f in enumerate(factors):
+    for q, f in enumerate(afac):
         V.memset(T.ca[:, q * P:(q + 1) * P], f).then_inc(S.fill, 1)
         fills += 1
     if fills:
         V.wait_ge(S.fill, fills)
-    if own_f not in (0, 1):
-        for c in range(NCH):
-            V.wait_ge(S["ldx%d" % c], 16)
-            V.tensor_tensor(T.xo[:, c * W:(c + 1) * W], T.xs[:, blk(k, c)], T.cx[:, c * W:(c + 1) * W],
-                            AluOpType.mult).then_inc(S["xo%d" % c], 1)
+    V.wait_ge(S.idy, 1)
+    for q, f in enumerate(ifac):
+        V.tensor_tensor(T.si[:, q * P:(q + 1) * P], T.idn[:], T.ci[:, q * P:(q + 1) * P],
+                        AluOpType.mult).then_inc(S.isc, 1)
     V.wait_ge(S.lda, 16)
-    for q, f in enumerate(factors):
+    for q, f in enumerate(afac):
         V.tensor_tensor(T.sa[:, q * P:(q + 1) * P], T.a0[:], T.ca[:, q * P:(q + 1) * P],
                         AluOpType.mult).then_inc(S.asc, 1)
+    for c in range(NQ):
+        V.wait_ge(S["vm%d" % c], 1)
+        V.tensor_copy(T.vs[:, blk(l, c)], T["pv%d" % c][:, 0:CW]).then_inc(S.vcp, 1)
 
+    g.wait_ge(S.one, 1)
+    g.affine_select(T.idn[:], T.on[:], [[-1, P]], AluOpType.is_equal, 0.0, 0, 1).then_inc(S.idy, 1)
     sent = 0
-    for c in range(NCH):
-        g.wait_ge(S["ldx%d" % c], 16)
-        sent += two_dests([m * G + l for m in col_others], [T.xs[:, blk(k, c)]], T.xs[:, blk(k, c)],
-                          S["p1c%d" % c], 0)
-    for c in range(NCH):
-        g.wait_ge(S["p1c%d" % c], p1_total)
-        srcs = []
-        if own_f == 1:
-            srcs.append(T.xs[:, blk(k, c)])
-        elif own_f != 0:
-            g.wait_ge(S["xo%d" % c], 1)
-            srcs.append(T.xo[:, c * W:(c + 1) * W])
-        for m in col_others:
-            srcs += [T.xs[:, blk(m, c)]] * (RA[tgt][m] // s_t)
-        sent += two_dests([tgt * G + j for j in row_others], srcs, T.vs[:, blk(l, c)], S["v%dc%d" % (l, c)], 1)
+    g.wait_ge(S.ldd, 16)
+    sent += write([m * G + l for m in col_next], T.xd[:], T.xs[:, slot(k)], S.p1)
+    g.wait_ge(S.vcp, NQ)
+    sent += write([k * G + j for j in row_next], T.vs[:, slot(l)], T.vs[:, slot(l)], S["v%d" % l])
 
     TE = g.tensor
+    TE.wait_ge(S.idy, 1)
+    if ifac:
+        TE.wait_ge(S.isc, len(ifac))
+    TE.wait_ge(S.ldx, 16)
+    for c in range(NQ):
+        TE.matmul(T["pv%d" % c][:, 0:CW], i_times(RA[k][k]), T.xs[:, blk(k, c)], True, False)
+    TE.wait_ge(S.p1, p1_total)
+    for n, m in enumerate(col_next):
+        last = n == len(col_next) - 1
+        for c in range(NQ):
+            mm = TE.matmul(T["pv%d" % c][:, 0:CW], i_times(RA[k][m]), T.xs[:, blk(m, c)], False, last)
+            if last:
+                mm.then_inc(S["vm%d" % c], 1)
     TE.wait_ge(S.lda, 16)
-    if factors:
-        TE.wait_ge(S.asc, len(factors))
-    for c in range(NCH):
-        ps = T["ps%d" % c]
-        TE.wait_ge(S["ldx%d" % c], 16)
-        TE.wait_ge(S["p1c%d" % c], p1_total)
-        for n, (f, m) in enumerate(own_terms):
-            TE.matmul(ps[:, 0:W], a_times(f), T.xs[:, blk(m, c)], n == 0, False)
-    for c in range(NCH):
-        ps = T["ps%d" % c]
-        for n, (f, j) in enumerate(in_terms):
-            TE.wait_ge(S["v%dc%d" % (j, c)], eng(src_row * G + j))
-            mm = TE.matmul(ps[:, 0:W], a_times(f), T.vs[:, blk(j, c)], False, n == len(in_terms) - 1)
-        mm.then_inc(S["mm%d" % c], 1)
+    if afac:
+        TE.wait_ge(S.asc, len(afac))
+    TE.wait_ge(S.vcp, NQ)
+    for c in range(NQ):
+        TE.matmul(T["ps%d" % c][:, 0:CW], a_times(CB[l][l]), T.vs[:, blk(l, c)], True, False)
+    for n, j in enumerate(row_from):
+        last = n == len(row_from) - 1
+        TE.wait_ge(S["v%d" % j], eng(k * G + j))
+        for c in range(NQ):
+            mm = TE.matmul(T["ps%d" % c][:, 0:CW], a_times(CB[l][j]), T.vs[:, blk(j, c)], False, last)
+            if last:
+                mm.then_inc(S["mm%d" % c], 1)
 
-    for c in range(NCH):
+    for c in range(NQ):
         V.wait_ge(S["mm%d" % c], 1)
-        V.tensor_copy(T.yb[:, c * W:(c + 1) * W], T["ps%d" % c][:, 0:W]).then_inc(S["cp%d" % c], 1)
-        q = ldq[c % 2]
-        q.wait_ge(S["cp%d" % c], 1)
-        q.dma_start(T.y[:, c * W:(c + 1) * W], T.yb[:, c * W:(c + 1) * W]).then_inc(S["st%d" % c], 16)
+        V.tensor_copy(T.yb[:, c * CW:(c + 1) * CW], T["ps%d" % c][:, 0:CW]).then_inc(S.cp, 1)
+    g.sync.wait_ge(S.cp, NQ)
+    g.sync.dma_start(T.y[:, 0:TK], T.yb[:]).then_inc(S.st, 16)
     g.wait_ge(S.sent, sent)
-    for c in range(NCH):
-        g.wait_ge(S["st%d" % c], 16)
+    g.wait_ge(S.st, 16)

@@ -19,14 +19,14 @@ SCRATCH = {
     "ca": ("sbuf", [P, G * P], "bfloat16"),
     "sa": ("sbuf", [P, G * P], "bfloat16"),
     "yb": ("sbuf", [P, TK], "bfloat16"),
+    "pv": ("psum", [P, 512], "float32"),
 }
 for _c in range(NQ):
-    SCRATCH["pv%d" % _c] = ("psum", [P, 512], "float32")
     SCRATCH["ps%d" % _c] = ("psum", [P, 512], "float32")
 
-SEMAPHORES = ["ldd", "ldx", "lda", "one", "fill", "idy", "isc", "asc", "sent", "p1", "vcp", "cp", "st"]
+SEMAPHORES = ["ldd", "ldx", "lda", "one", "fill", "idy", "isc", "asc", "sent", "vm", "vcp", "cp", "st"]
+SEMAPHORES += ["xa%d" % _l for _l in range(G)]
 SEMAPHORES += ["v%d" % _l for _l in range(G)]
-SEMAPHORES += ["vm%d" % _c for _c in range(NQ)]
 SEMAPHORES += ["mm%d" % _c for _c in range(NQ)]
 
 
@@ -60,25 +60,37 @@ def rank_program(g, core, T, topo):
         return bin(topo.mask(T.cores[src_rank], core)).count("1")
 
     col_next = [(k + 1) % G, (k + 2) % G]
+    m_early, m_late = (k + G - 1) % G, (k + 1) % G
     row_next = [(l + 1) % G, (l + 2) % G]
     row_from = [(l + G - 1) % G, (l + 1) % G]
-    p1_total = sum(eng(m * G + l) for m in col_next)
+
+    d_late = RA[k][m_late]
+    direct = d_late != 0 and (abs(d_late) & (abs(d_late) - 1)) == 0
+    div = d_late if direct else 1
+    te_terms = [k, m_early] if direct else [k, m_early, m_late]
+
+    def ic(m):
+        return float(RA[k][m]) / float(div)
+
+    def ac(j):
+        return float(CB[l][j] * div)
 
     ifac, afac = [], []
-    for m in range(G):
-        if RA[k][m] != 1 and RA[k][m] not in ifac:
-            ifac.append(RA[k][m])
-        if CB[l][m] != 1 and CB[l][m] not in afac:
-            afac.append(CB[l][m])
+    for m in te_terms:
+        if ic(m) != 1.0 and ic(m) not in ifac:
+            ifac.append(ic(m))
+    for j in range(G):
+        if ac(j) != 1.0 and ac(j) not in afac:
+            afac.append(ac(j))
 
     def i_times(f):
-        if f == 1:
+        if f == 1.0:
             return T.idn[:]
         q = ifac.index(f)
         return T.si[:, q * P:(q + 1) * P]
 
     def a_times(f):
-        if f == 1:
+        if f == 1.0:
             return T.a0[:]
         q = afac.index(f)
         return T.sa[:, q * P:(q + 1) * P]
@@ -106,16 +118,19 @@ def rank_program(g, core, T, topo):
     for q, f in enumerate(afac):
         V.tensor_tensor(T.sa[:, q * P:(q + 1) * P], T.a0[:], T.ca[:, q * P:(q + 1) * P],
                         AluOpType.mult).then_inc(S.asc, 1)
-    for c in range(NQ):
-        V.wait_ge(S["vm%d" % c], 1)
-        V.tensor_copy(T.vs[:, blk(l, c)], T["pv%d" % c][:, 0:CW]).then_inc(S.vcp, 1)
+    V.wait_ge(S.vm, 1)
+    if direct:
+        V.wait_ge(S["xa%d" % m_late], eng(m_late * G + l))
+        V.tensor_tensor(T.vs[:, slot(l)], T.pv[:, 0:TK], T.xs[:, slot(m_late)], AluOpType.add).then_inc(S.vcp, 1)
+    else:
+        V.tensor_copy(T.vs[:, slot(l)], T.pv[:, 0:TK]).then_inc(S.vcp, 1)
 
-    g.wait_ge(S.one, 1)
-    g.affine_select(T.idn[:], T.on[:], [[-1, P]], AluOpType.is_equal, 0.0, 0, 1).then_inc(S.idy, 1)
     sent = 0
     g.wait_ge(S.ldd, 16)
-    sent += write([m * G + l for m in col_next], T.xd[:], T.xs[:, slot(k)], S.p1)
-    g.wait_ge(S.vcp, NQ)
+    sent += write([m * G + l for m in col_next], T.xd[:], T.xs[:, slot(k)], S["xa%d" % k])
+    g.wait_ge(S.one, 1)
+    g.affine_select(T.idn[:], T.on[:], [[-1, P]], AluOpType.is_equal, 0.0, 0, 1).then_inc(S.idy, 1)
+    g.wait_ge(S.vcp, 1)
     sent += write([k * G + j for j in row_next], T.vs[:, slot(l)], T.vs[:, slot(l)], S["v%d" % l])
 
     TE = g.tensor
@@ -123,26 +138,24 @@ def rank_program(g, core, T, topo):
     if ifac:
         TE.wait_ge(S.isc, len(ifac))
     TE.wait_ge(S.ldx, 16)
-    for c in range(NQ):
-        TE.matmul(T["pv%d" % c][:, 0:CW], i_times(RA[k][k]), T.xs[:, blk(k, c)], True, False)
-    TE.wait_ge(S.p1, p1_total)
-    for n, m in enumerate(col_next):
-        last = n == len(col_next) - 1
-        for c in range(NQ):
-            mm = TE.matmul(T["pv%d" % c][:, 0:CW], i_times(RA[k][m]), T.xs[:, blk(m, c)], False, last)
-            if last:
-                mm.then_inc(S["vm%d" % c], 1)
+    for n, m in enumerate(te_terms):
+        last = n == len(te_terms) - 1
+        if m != k:
+            TE.wait_ge(S["xa%d" % m], eng(m * G + l))
+        mm = TE.matmul(T.pv[:, 0:TK], i_times(ic(m)), T.xs[:, slot(m)], n == 0, last)
+        if last:
+            mm.then_inc(S.vm, 1)
     TE.wait_ge(S.lda, 16)
     if afac:
         TE.wait_ge(S.asc, len(afac))
-    TE.wait_ge(S.vcp, NQ)
+    TE.wait_ge(S.vcp, 1)
     for c in range(NQ):
-        TE.matmul(T["ps%d" % c][:, 0:CW], a_times(CB[l][l]), T.vs[:, blk(l, c)], True, False)
+        TE.matmul(T["ps%d" % c][:, 0:CW], a_times(ac(l)), T.vs[:, blk(l, c)], True, False)
     for n, j in enumerate(row_from):
         last = n == len(row_from) - 1
         TE.wait_ge(S["v%d" % j], eng(k * G + j))
         for c in range(NQ):
-            mm = TE.matmul(T["ps%d" % c][:, 0:CW], a_times(CB[l][j]), T.vs[:, blk(j, c)], False, last)
+            mm = TE.matmul(T["ps%d" % c][:, 0:CW], a_times(ac(j)), T.vs[:, blk(j, c)], False, last)
             if last:
                 mm.then_inc(S["mm%d" % c], 1)
 

@@ -4,11 +4,11 @@ from concourse.mybir import AluOpType
 P = 128
 TK = 512
 G = 3
-NQ = 4
-CW = TK // NQ
+NB = 2
+HW = TK // NB
+YB = [[(0, HW)], [(HW, HW // 2), (HW + HW // 2, HW // 2)]]
 
 SCRATCH = {
-    "xd": ("dram", [P, TK], "bfloat16"),
     "xs": ("sbuf", [P, G * TK], "bfloat16"),
     "vs": ("sbuf", [P, G * TK], "bfloat16"),
     "on": ("sbuf", [P, P], "bfloat16"),
@@ -19,15 +19,16 @@ SCRATCH = {
     "ca": ("sbuf", [P, G * P], "bfloat16"),
     "sa": ("sbuf", [P, G * P], "bfloat16"),
     "yb": ("sbuf", [P, TK], "bfloat16"),
-    "pv": ("psum", [P, 512], "float32"),
 }
-for _c in range(NQ):
-    SCRATCH["ps%d" % _c] = ("psum", [P, 512], "float32")
-
-SEMAPHORES = ["ldd", "ldx", "lda", "one", "fill", "idy", "isc", "asc", "sent", "vm", "vcp", "cp", "st"]
-SEMAPHORES += ["xa%d" % _l for _l in range(G)]
-SEMAPHORES += ["v%d" % _l for _l in range(G)]
-SEMAPHORES += ["mm%d" % _c for _c in range(NQ)]
+SEMAPHORES = ["lda", "one", "fill", "idy", "isc", "asc", "sent"]
+for _b in range(NB):
+    SCRATCH["pv%d" % _b] = ("psum", [P, 512], "float32")
+    SEMAPHORES += ["ldx%d" % _b, "vm%d" % _b, "vcp%d" % _b, "cp%d" % _b, "st%d" % _b]
+    SEMAPHORES += ["xa%d_%d" % (_l, _b) for _l in range(G)]
+    SEMAPHORES += ["v%d_%d" % (_l, _b) for _l in range(G)]
+    for _c in range(len(YB[_b])):
+        SCRATCH["ps%d_%d" % (_b, _c)] = ("psum", [P, 512], "float32")
+        SEMAPHORES += ["mm%d_%d" % (_b, _c)]
 
 
 def rank_program(g, core, T, topo):
@@ -38,21 +39,21 @@ def rank_program(g, core, T, topo):
     S = T.sem
     k, l = rank // G, rank % G
 
-    def slot(q):
-        return slice(q * TK, (q + 1) * TK)
+    def cols(q, off, w):
+        return slice(q * TK + off, q * TK + off + w)
 
-    def blk(q, c):
-        return slice(q * TK + c * CW, q * TK + (c + 1) * CW)
+    def half(q, b):
+        return cols(q, b * HW, HW)
 
-    def write(ranks, src, dst_ap, sem):
+    def write(ranks, ap, sem):
         cores = [T.cores[r] for r in ranks]
         mask = -1
         for d in cores:
             assert topo.may_write(core, d)
             mask &= topo.mask(core, d)
         ids = [DstId(rid=topo.addr(d)[0], pnc=topo.addr(d)[1]) for d in cores]
-        tr = RemoteDMATransfer(dst_ids=ids, dma_engine_mask=mask, remote_sem=sem, srcs=[src],
-                               dsts=[dst_ap for _ in cores], alu_op=0)
+        tr = RemoteDMATransfer(dst_ids=ids, dma_engine_mask=mask, remote_sem=sem, srcs=[ap],
+                               dsts=[ap for _ in cores], alu_op=0)
         g.remote_dma_fused([tr], local_sem=S.sent)
         return bin(mask).count("1")
 
@@ -95,8 +96,8 @@ def rank_program(g, core, T, topo):
         q = afac.index(f)
         return T.sa[:, q * P:(q + 1) * P]
 
-    g.sync.dma_start(T.xd[:], T.x[:, 0:TK]).then_inc(S.ldd, 16)
-    g.sync.dma_start(T.xs[:, slot(k)], T.x[:, 0:TK]).then_inc(S.ldx, 16)
+    for b in range(NB):
+        g.sync.dma_start(T.xs[:, half(k, b)], T.x[:, b * HW:(b + 1) * HW]).then_inc(S["ldx%d" % b], 16)
     g.sync.dma_start(T.a0[:], T.a[:]).then_inc(S.lda, 16)
 
     V = g.vector
@@ -118,51 +119,63 @@ def rank_program(g, core, T, topo):
     for q, f in enumerate(afac):
         V.tensor_tensor(T.sa[:, q * P:(q + 1) * P], T.a0[:], T.ca[:, q * P:(q + 1) * P],
                         AluOpType.mult).then_inc(S.asc, 1)
-    V.wait_ge(S.vm, 1)
-    if direct:
-        V.wait_ge(S["xa%d" % m_late], eng(m_late * G + l))
-        V.tensor_tensor(T.vs[:, slot(l)], T.pv[:, 0:TK], T.xs[:, slot(m_late)], AluOpType.add).then_inc(S.vcp, 1)
-    else:
-        V.tensor_copy(T.vs[:, slot(l)], T.pv[:, 0:TK]).then_inc(S.vcp, 1)
+    for b in range(NB):
+        V.wait_ge(S["vm%d" % b], 1)
+        if direct:
+            V.wait_ge(S["xa%d_%d" % (m_late, b)], eng(m_late * G + l))
+            V.tensor_tensor(T.vs[:, half(l, b)], T["pv%d" % b][:, 0:HW], T.xs[:, half(m_late, b)],
+                            AluOpType.add).then_inc(S["vcp%d" % b], 1)
+        else:
+            V.tensor_copy(T.vs[:, half(l, b)], T["pv%d" % b][:, 0:HW]).then_inc(S["vcp%d" % b], 1)
 
     sent = 0
-    g.wait_ge(S.ldd, 16)
-    sent += write([m * G + l for m in col_next], T.xd[:], T.xs[:, slot(k)], S["xa%d" % k])
+    for b in range(NB):
+        g.wait_ge(S["ldx%d" % b], 16)
+        sent += write([m * G + l for m in col_next], T.xs[:, half(k, b)], S["xa%d_%d" % (k, b)])
     g.wait_ge(S.one, 1)
     g.affine_select(T.idn[:], T.on[:], [[-1, P]], AluOpType.is_equal, 0.0, 0, 1).then_inc(S.idy, 1)
-    g.wait_ge(S.vcp, 1)
-    sent += write([k * G + j for j in row_next], T.vs[:, slot(l)], T.vs[:, slot(l)], S["v%d" % l])
+    for b in range(NB):
+        g.wait_ge(S["vcp%d" % b], 1)
+        sent += write([k * G + j for j in row_next], T.vs[:, half(l, b)], S["v%d_%d" % (l, b)])
 
     TE = g.tensor
     TE.wait_ge(S.idy, 1)
     if ifac:
         TE.wait_ge(S.isc, len(ifac))
-    TE.wait_ge(S.ldx, 16)
-    for n, m in enumerate(te_terms):
-        last = n == len(te_terms) - 1
-        if m != k:
-            TE.wait_ge(S["xa%d" % m], eng(m * G + l))
-        mm = TE.matmul(T.pv[:, 0:TK], i_times(ic(m)), T.xs[:, slot(m)], n == 0, last)
-        if last:
-            mm.then_inc(S.vm, 1)
+    for b in range(NB):
+        TE.wait_ge(S["ldx%d" % b], 16)
+        TE.matmul(T["pv%d" % b][:, 0:HW], i_times(ic(k)), T.xs[:, half(k, b)], True, False)
+    for b in range(NB):
+        for n, m in enumerate(te_terms):
+            if m == k:
+                continue
+            last = n == len(te_terms) - 1
+            TE.wait_ge(S["xa%d_%d" % (m, b)], eng(m * G + l))
+            mm = TE.matmul(T["pv%d" % b][:, 0:HW], i_times(ic(m)), T.xs[:, half(m, b)], False, last)
+            if last:
+                mm.then_inc(S["vm%d" % b], 1)
     TE.wait_ge(S.lda, 16)
     if afac:
         TE.wait_ge(S.asc, len(afac))
-    TE.wait_ge(S.vcp, 1)
-    for c in range(NQ):
-        TE.matmul(T["ps%d" % c][:, 0:CW], a_times(ac(l)), T.vs[:, blk(l, c)], True, False)
-    for n, j in enumerate(row_from):
-        last = n == len(row_from) - 1
-        TE.wait_ge(S["v%d" % j], eng(k * G + j))
-        for c in range(NQ):
-            mm = TE.matmul(T["ps%d" % c][:, 0:CW], a_times(ac(j)), T.vs[:, blk(j, c)], False, last)
-            if last:
-                mm.then_inc(S["mm%d" % c], 1)
+    for b in range(NB):
+        TE.wait_ge(S["vcp%d" % b], 1)
+        for c, (off, w) in enumerate(YB[b]):
+            TE.matmul(T["ps%d_%d" % (b, c)][:, 0:w], a_times(ac(l)), T.vs[:, cols(l, off, w)], True, False)
+    for b in range(NB):
+        for n, j in enumerate(row_from):
+            last = n == len(row_from) - 1
+            TE.wait_ge(S["v%d_%d" % (j, b)], eng(k * G + j))
+            for c, (off, w) in enumerate(YB[b]):
+                mm = TE.matmul(T["ps%d_%d" % (b, c)][:, 0:w], a_times(ac(j)), T.vs[:, cols(j, off, w)], False, last)
+                if last:
+                    mm.then_inc(S["mm%d_%d" % (b, c)], 1)
 
-    for c in range(NQ):
-        V.wait_ge(S["mm%d" % c], 1)
-        V.tensor_copy(T.yb[:, c * CW:(c + 1) * CW], T["ps%d" % c][:, 0:CW]).then_inc(S.cp, 1)
-    g.sync.wait_ge(S.cp, NQ)
-    g.sync.dma_start(T.y[:, 0:TK], T.yb[:]).then_inc(S.st, 16)
+    for b in range(NB):
+        for c, (off, w) in enumerate(YB[b]):
+            V.wait_ge(S["mm%d_%d" % (b, c)], 1)
+            V.tensor_copy(T.yb[:, off:off + w], T["ps%d_%d" % (b, c)][:, 0:w]).then_inc(S["cp%d" % b], 1)
+        g.sync.wait_ge(S["cp%d" % b], len(YB[b]))
+        g.sync.dma_start(T.y[:, b * HW:(b + 1) * HW], T.yb[:, b * HW:(b + 1) * HW]).then_inc(S["st%d" % b], 16)
     g.wait_ge(S.sent, sent)
-    g.wait_ge(S.st, 16)
+    for b in range(NB):
+        g.wait_ge(S["st%d" % b], 16)

from concourse.bass import DstId, RemoteDMATransfer
from concourse.mybir import AluOpType

P = 128
TK = 512
G = 3
NB = 2
HW = TK // NB
YB = [[(0, HW)], [(HW, HW // 2), (HW + HW // 2, HW // 2)]]

SCRATCH = {
    "xs": ("sbuf", [P, G * TK], "bfloat16"),
    "vs": ("sbuf", [P, G * TK], "bfloat16"),
    "on": ("sbuf", [P, P], "bfloat16"),
    "idn": ("sbuf", [P, P], "bfloat16"),
    "ci": ("sbuf", [P, G * P], "bfloat16"),
    "si": ("sbuf", [P, G * P], "bfloat16"),
    "a0": ("sbuf", [P, P], "bfloat16"),
    "ca": ("sbuf", [P, G * P], "bfloat16"),
    "sa": ("sbuf", [P, G * P], "bfloat16"),
    "yb": ("sbuf", [P, TK], "bfloat16"),
}
SEMAPHORES = ["lda", "one", "fill", "idy", "isc", "asc", "sent"]
for _b in range(NB):
    SCRATCH["pv%d" % _b] = ("psum", [P, 512], "float32")
    SEMAPHORES += ["ldx%d" % _b, "vm%d" % _b, "vcp%d" % _b, "cp%d" % _b, "st%d" % _b]
    SEMAPHORES += ["xa%d_%d" % (_l, _b) for _l in range(G)]
    SEMAPHORES += ["v%d_%d" % (_l, _b) for _l in range(G)]
    for _c in range(len(YB[_b])):
        SCRATCH["ps%d_%d" % (_b, _c)] = ("psum", [P, 512], "float32")
        SEMAPHORES += ["mm%d_%d" % (_b, _c)]


def rank_program(g, core, T, topo):
    rank = T.rank_of(core)
    if rank is None:
        return
    RA, CB = T.tables["RA"], T.tables["CB"]
    S = T.sem
    k, l = rank // G, rank % G

    def cols(q, off, w):
        return slice(q * TK + off, q * TK + off + w)

    def half(q, b):
        return cols(q, b * HW, HW)

    def write(ranks, ap, sem):
        cores = [T.cores[r] for r in ranks]
        mask = -1
        for d in cores:
            assert topo.may_write(core, d)
            mask &= topo.mask(core, d)
        ids = [DstId(rid=topo.addr(d)[0], pnc=topo.addr(d)[1]) for d in cores]
        tr = RemoteDMATransfer(dst_ids=ids, dma_engine_mask=mask, remote_sem=sem, srcs=[ap],
                               dsts=[ap for _ in cores], alu_op=0)
        g.remote_dma_fused([tr], local_sem=S.sent)
        return bin(mask).count("1")

    def eng(src_rank):
        return bin(topo.mask(T.cores[src_rank], core)).count("1")

    col_next = [(k + 1) % G, (k + 2) % G]
    m_early, m_late = (k + G - 1) % G, (k + 1) % G
    row_next = [(l + 1) % G, (l + 2) % G]
    row_from = [(l + G - 1) % G, (l + 1) % G]

    d_late = RA[k][m_late]
    direct = d_late != 0 and (abs(d_late) & (abs(d_late) - 1)) == 0
    div = d_late if direct else 1
    te_terms = [k, m_early] if direct else [k, m_early, m_late]

    def ic(m):
        return float(RA[k][m]) / float(div)

    def ac(j):
        return float(CB[l][j] * div)

    ifac, afac = [], []
    for m in te_terms:
        if ic(m) != 1.0 and ic(m) not in ifac:
            ifac.append(ic(m))
    for j in range(G):
        if ac(j) != 1.0 and ac(j) not in afac:
            afac.append(ac(j))

    def i_times(f):
        if f == 1.0:
            return T.idn[:]
        q = ifac.index(f)
        return T.si[:, q * P:(q + 1) * P]

    def a_times(f):
        if f == 1.0:
            return T.a0[:]
        q = afac.index(f)
        return T.sa[:, q * P:(q + 1) * P]

    for b in range(NB):
        g.sync.dma_start(T.xs[:, half(k, b)], T.x[:, b * HW:(b + 1) * HW]).then_inc(S["ldx%d" % b], 16)
    g.sync.dma_start(T.a0[:], T.a[:]).then_inc(S.lda, 16)

    V = g.vector
    V.memset(T.on[:], 1.0).then_inc(S.one, 1)
    fills = 0
    for q, f in enumerate(ifac):
        V.memset(T.ci[:, q * P:(q + 1) * P], f).then_inc(S.fill, 1)
        fills += 1
    for q, f in enumerate(afac):
        V.memset(T.ca[:, q * P:(q + 1) * P], f).then_inc(S.fill, 1)
        fills += 1
    if fills:
        V.wait_ge(S.fill, fills)
    V.wait_ge(S.idy, 1)
    for q, f in enumerate(ifac):
        V.tensor_tensor(T.si[:, q * P:(q + 1) * P], T.idn[:], T.ci[:, q * P:(q + 1) * P],
                        AluOpType.mult).then_inc(S.isc, 1)
    V.wait_ge(S.lda, 16)
    for q, f in enumerate(afac):
        V.tensor_tensor(T.sa[:, q * P:(q + 1) * P], T.a0[:], T.ca[:, q * P:(q + 1) * P],
                        AluOpType.mult).then_inc(S.asc, 1)
    for b in range(NB):
        V.wait_ge(S["vm%d" % b], 1)
        if direct:
            V.wait_ge(S["xa%d_%d" % (m_late, b)], eng(m_late * G + l))
            V.tensor_tensor(T.vs[:, half(l, b)], T["pv%d" % b][:, 0:HW], T.xs[:, half(m_late, b)],
                            AluOpType.add).then_inc(S["vcp%d" % b], 1)
        else:
            V.tensor_copy(T.vs[:, half(l, b)], T["pv%d" % b][:, 0:HW]).then_inc(S["vcp%d" % b], 1)

    sent = 0
    for b in range(NB):
        g.wait_ge(S["ldx%d" % b], 16)
        sent += write([m * G + l for m in col_next], T.xs[:, half(k, b)], S["xa%d_%d" % (k, b)])
    g.wait_ge(S.one, 1)
    g.affine_select(T.idn[:], T.on[:], [[-1, P]], AluOpType.is_equal, 0.0, 0, 1).then_inc(S.idy, 1)
    for b in range(NB):
        g.wait_ge(S["vcp%d" % b], 1)
        sent += write([k * G + j for j in row_next], T.vs[:, half(l, b)], S["v%d_%d" % (l, b)])

    TE = g.tensor
    TE.wait_ge(S.idy, 1)
    if ifac:
        TE.wait_ge(S.isc, len(ifac))
    for b in range(NB):
        TE.wait_ge(S["ldx%d" % b], 16)
        TE.matmul(T["pv%d" % b][:, 0:HW], i_times(ic(k)), T.xs[:, half(k, b)], True, False)
    for b in range(NB):
        for n, m in enumerate(te_terms):
            if m == k:
                continue
            last = n == len(te_terms) - 1
            TE.wait_ge(S["xa%d_%d" % (m, b)], eng(m * G + l))
            mm = TE.matmul(T["pv%d" % b][:, 0:HW], i_times(ic(m)), T.xs[:, half(m, b)], False, last)
            if last:
                mm.then_inc(S["vm%d" % b], 1)
    TE.wait_ge(S.lda, 16)
    if afac:
        TE.wait_ge(S.asc, len(afac))
    for b in range(NB):
        TE.wait_ge(S["vcp%d" % b], 1)
        for c, (off, w) in enumerate(YB[b]):
            TE.matmul(T["ps%d_%d" % (b, c)][:, 0:w], a_times(ac(l)), T.vs[:, cols(l, off, w)], True, False)
    for b in range(NB):
        for n, j in enumerate(row_from):
            last = n == len(row_from) - 1
            TE.wait_ge(S["v%d_%d" % (j, b)], eng(k * G + j))
            for c, (off, w) in enumerate(YB[b]):
                mm = TE.matmul(T["ps%d_%d" % (b, c)][:, 0:w], a_times(ac(j)), T.vs[:, cols(j, off, w)], False, last)
                if last:
                    mm.then_inc(S["mm%d_%d" % (b, c)], 1)

    for b in range(NB):
        for c, (off, w) in enumerate(YB[b]):
            V.wait_ge(S["mm%d_%d" % (b, c)], 1)
            V.tensor_copy(T.yb[:, off:off + w], T["ps%d_%d" % (b, c)][:, 0:w]).then_inc(S["cp%d" % b], 1)
        g.sync.wait_ge(S["cp%d" % b], len(YB[b]))
        g.sync.dma_start(T.y[:, b * HW:(b + 1) * HW], T.yb[:, b * HW:(b + 1) * HW]).then_inc(S["st%d" % b], 16)
    g.wait_ge(S.sent, sent)
    for b in range(NB):
        g.wait_ge(S["st%d" % b], 16)
